import numpy as np
import ml_dtypes


def mxq(x, axis, fmt="e4m3"):
    dtype, down = {"e4m3": (ml_dtypes.float8_e4m3fn, 7), "e5m2": (ml_dtypes.float8_e5m2, 14)}[fmt]
    v = np.moveaxis(np.asarray(x, np.float32).astype(ml_dtypes.bfloat16).astype(np.float64), axis, -1)
    blocks = v.reshape(v.shape[:-1] + (-1, 32))
    amax = np.abs(blocks).max(-1, keepdims=True)
    byte = np.maximum(np.where(amax > 0, np.frexp(amax)[1] - 1 + 127, 0) - down, 1)
    scale = np.exp2(byte - 127.0)
    codes = (blocks / scale).astype(np.float32).astype(dtype).astype(np.float64)
    return np.moveaxis((codes * scale).reshape(v.shape), -1, axis)


WIDE = False


def mx_kscale(k):
    if not WIDE:
        return np.ones(k)
    levels = np.array([10, -10, 5, -5, 0])
    if k % 512:
        return np.exp2(np.random.permutation(np.resize(levels, k // 32))).repeat(32)
    a = np.empty((k // 512, 16))
    for p in range(k // 512):
        a[p, :8] = np.random.permutation(np.resize(levels, 8))
        for g in range(8):
            far = levels[np.abs(levels - a[p, g]) >= 10]
            a[p, g + 8] = far[np.random.randint(len(far))]
    return np.exp2(a.ravel()).repeat(32)


def f64(x):
    return np.asarray(x).astype(np.float64)


def striped(idx):
    return np.tile(np.asarray(idx).reshape(-1, 16).T, (8, 1)).astype(np.uint16)


def unstriped(offs):
    return offs[:16].T.reshape(-1).astype(np.int64)


E2M1 = np.array([0.0, 0.5, 1.0, 1.5, 2.0, 3.0, 4.0, 6.0, -0.0, -0.5, -1.0, -1.5, -2.0, -3.0, -4.0, -6.0])


def pack_weight(w, fmt):
    k, n = w.shape
    w = f64(np.asarray(w, np.float32).astype(ml_dtypes.bfloat16)).reshape(k // 32, 32, n)
    amax = np.abs(w).max(1)
    if fmt == "e4m3":
        byte = np.frexp(amax)[1] - 1 + 127 - 7
    else:
        mant, ex = np.frexp(amax / 6.0)
        byte = np.where(mant > 0.5, ex, ex - 1) + 127
    byte = np.clip(np.where(amax > 0, byte, 1), 1, 254)
    scaled = (w * np.exp2(127.0 - byte)[:, None, :]).reshape(k, n).astype(np.float32)
    by_word = np.ascontiguousarray(scaled.reshape(k // 512, 128, 4, n).transpose(0, 1, 3, 2))
    if fmt == "e4m3":
        words = by_word.astype(ml_dtypes.float8_e4m3fn).view(np.uint8)
    else:
        c = by_word.astype(ml_dtypes.float4_e2m1fn).view(np.uint8) & 0xF
        words = (c[..., 0::2] | (c[..., 1::2] << 4)).reshape(k // 512, 128, 2 * n)
    return np.ascontiguousarray(words), np.ascontiguousarray(byte.astype(np.uint8).reshape(k // 512, 16, n))


def unpack_weight(words, scales, fmt):
    g, _, n = scales.shape
    words = np.ascontiguousarray(words).reshape(g, 128, n, -1)
    if fmt == "e4m3":
        vals = words.view(ml_dtypes.float8_e4m3fn).astype(np.float64)
    else:
        nib = np.empty((g, 128, n, 4), np.uint8)
        nib[..., 0::2] = words & 0xF
        nib[..., 1::2] = words >> 4
        vals = E2M1[nib]
    vals = vals * np.repeat(np.exp2(scales.astype(np.float64) - 127.0), 8, axis=1)[..., None]
    return vals.transpose(0, 1, 3, 2).reshape(g * 512, n)


def bf(x):
    return np.asarray(x, np.float32).astype(ml_dtypes.bfloat16)


def planes(Y):
    r, m = Y.shape
    b = f64(bf(Y)).reshape(r // 32, 32, m)
    amax = np.abs(b).max(1)
    byte = np.clip(np.where(amax > 0, np.frexp(amax)[1] - 1 + 127 - 7, 1), 1, 254)
    codes = (b * np.exp2(127.0 - byte)[:, None, :]).reshape(r, m).astype(np.float32).astype(ml_dtypes.float8_e4m3fn).view(np.uint8)
    words = codes.reshape(r // 512, 128, 4, m).transpose(0, 1, 3, 2)
    return np.ascontiguousarray(words), np.ascontiguousarray(byte.astype(np.uint8).reshape(r // 512, 16, m))


K, T, J, I, N, M = 1024, 1024, 512, 512, 512, 512


def setup_inputs():
    n = np.random.standard_normal
    idx = np.random.permutation(T)[:J]
    idx2 = np.random.permutation(T)[:I]
    fk = mx_kscale(K)
    fn = mx_kscale(N)
    xtp = pack_weight(n((K, T)) / fk[:, None], "e2m1")
    wap = pack_weight(n((K, N)) * 1 / np.sqrt(K) * fk[:, None] * fn, "e4m3")
    wbp = pack_weight(n((K, N)) * 1 / np.sqrt(K) * fk[:, None] * fn, "e2m1")
    wmp = pack_weight(n((N, M)) * 1 / np.sqrt(N) / fn[:, None], "e4m3")
    return {
        "xt_words": xtp[0],
        "xt_scales": xtp[1],
        "wa_words": wap[0],
        "wa_scales": wap[1],
        "wb_words": wbp[0],
        "wb_scales": wbp[1],
        "res": (n((N, T)) * 0.5 * fn[:, None]).astype(np.float32),
        "wm_words": wmp[0],
        "wm_scales": wmp[1],
        "ga": (np.random.uniform(0.4, 1.2, (1, J))).astype(np.float32),
        "gb": (np.random.uniform(0.4, 1.2, (1, I))).astype(np.float32),
        "offs": striped(idx),
        "offs2": striped(idx2),
    }


def reference(xt_words, xt_scales, wa_words, wa_scales, wb_words, wb_scales, res, wm_words, wm_scales, ga, gb, offs, offs2):
    idx = unstriped(offs)
    idx2 = unstriped(offs2)
    xtu = unpack_weight(xt_words, xt_scales, "e2m1")
    wau = unpack_weight(wa_words, wa_scales, "e4m3")
    wbu = unpack_weight(wb_words, wb_scales, "e2m1")
    wmu = unpack_weight(wm_words, wm_scales, "e4m3")
    xtidxg = xtu[:, idx]
    p = wau.T @ xtidxg
    xtidx2g = xtu[:, idx2]
    q = wbu.T @ xtidx2g
    pw = p * f64(ga)
    qw = q * f64(gb)
    pg = np.zeros((N, T))
    pg[:, idx] = pw
    qg = np.zeros((N, T))
    qg[:, idx2] = qw
    h1 = np.maximum(pg + qg + f64(res), 0.0)
    h1q = mxq(h1, 0, "e4m3")
    y = wmu.T @ h1q
    words, scales = planes(y)
    return y, words, scales

@@ -1,0 +1,274 @@
+from contextlib import ExitStack
+
+import concourse.mybir as mybir
+from concourse.masks import make_identity
+
+K, T, J, N, M = 1024, 1024, 512, 512, 512
+FLOPS = 2 * (2 * K * N * J + N * M * T)
+
+F32 = mybir.dt.float32
+BF16 = mybir.dt.bfloat16
+I32 = mybir.dt.int32
+U16 = mybir.dt.uint16
+U8 = mybir.dt.uint8
+FP8X4 = mybir.dt.float8_e4m3fn_x4
+FP4X4 = mybir.dt.float4_e2m1fn_x4
+ADD = mybir.AluOpType.add
+MAX = mybir.AluOpType.max
+COPY = mybir.ActivationFunctionType.Copy
+RELU = mybir.ActivationFunctionType.Relu
+
+P = 128
+PACK = 4
+PASSES = 2
+QUADS = 4
+CHUNK = 256
+CHUNKS = T // CHUNK
+
+
+def tile_moe_experts_then_shared_layer_pl_kernel(
+    tc, xt_words, xt_scales, wa_words, wa_scales, wb_words, wb_scales, res, wm_words, wm_scales, ga, gb, offs, offs2,
+    out_0, out_1, out_2,
+):
+    nc = tc.nc
+    with ExitStack() as ctx:
+        sb = ctx.enter_context(tc.tile_pool(name="sb", bufs=1))
+        ps = ctx.enter_context(tc.psum_pool(name="ps", bufs=1))
+
+        def tile(name, shape, dtype):
+            return sb.tile(shape, dtype, name=name, align_bytes=64)
+
+        def bank(name, tag, shape):
+            return ps.tile(shape, F32, name=name, tag=tag)
+
+        def zeroed_plane(name, shape):
+            plane = tile(name, shape, U8)
+            nc.vector.memset(plane[:].bitcast(I32), 0)
+            return plane
+
+        def load_weight_scales(plane, scales):
+            for q in range(QUADS):
+                nc.sync.dma_start(
+                    out=plane[32 * q : 32 * q + 4, :, :].bitcast(I32),
+                    in_=scales[:, 4 * q : 4 * q + 4, :].rearrange("a r n -> r a n").bitcast(I32),
+                )
+
+        lists = [tile("list_a", [P, J // 16], U16), tile("list_b", [P, J // 16], U16)]
+        xs = zeroed_plane("xs", [P, T])
+        was = zeroed_plane("was", [P, PASSES, N])
+        moved = [zeroed_plane("moved_a", [P, J]), zeroed_plane("moved_b", [P, J])]
+        wms = zeroed_plane("wms", [P, 1, M])
+        wbs = zeroed_plane("wbs", [P, PASSES, N])
+
+        ident = tile("ident", [P, P], F32)
+        make_identity(nc, ident[:])
+        windows = [[tile("win%d%d" % (e, b), [P, T], F32) for b in range(2)] for e in range(2)]
+        for e in range(2):
+            for b in range(2):
+                nc.gpsimd.memset(windows[e][b][:], 0.0)
+
+        nc.sync.dma_start(lists[0][:], offs)
+        for q in range(QUADS):
+            nc.sync.dma_start(
+                out=xs[32 * q : 32 * q + 8, :].bitcast(I32),
+                in_=xt_scales[:, 4 * q : 4 * q + 4, :].bitcast(I32),
+            )
+        xw = []
+        for a in range(PASSES):
+            w = tile("xw%d" % a, [P, T], U16)
+            nc.sync.dma_start(out=w[:].bitcast(I32), in_=xt_words[a].bitcast(I32))
+            xw.append(w)
+        nc.sync.dma_start(lists[1][:], offs2)
+        load_weight_scales(was, wa_scales)
+        wa = []
+        for a in range(PASSES):
+            w = tile("wa%d" % a, [P, N], I32)
+            nc.sync.dma_start(out=w[:], in_=wa_words[a].rearrange("p n t -> p (n t)").bitcast(I32))
+            wa.append(w)
+        gates = [tile("gate_a", [P, J // P], F32), tile("gate_b", [P, J // P], F32)]
+        with nc.allow_non_contiguous_dma(reason="one gate to a partition"):
+            nc.sync.dma_start(out=gates[0][:], in_=ga.rearrange("o (c p) -> p (o c)", p=P))
+        wm = tile("wm", [P, M], I32)
+        nc.sync.dma_start(out=wm[:], in_=wm_words[0].rearrange("p n t -> p (n t)").bitcast(I32))
+        load_weight_scales(wms, wm_scales)
+        load_weight_scales(wbs, wb_scales)
+        wb = tile("wb", [P, PASSES, N // 2], I32)
+        nc.sync.dma_start(out=wb[:], in_=wb_words.rearrange("a p n -> p a n").bitcast(I32))
+        with nc.allow_non_contiguous_dma(reason="one gate to a partition"):
+            nc.sync.dma_start(out=gates[1][:], in_=gb.rearrange("o (c p) -> p (o c)", p=P))
+        sums = []
+        res_rows = res.rearrange("(p s) t -> p s t", s=PACK)
+        for s in range(PACK):
+            r = tile("res%d" % s, [P, T], F32)
+            nc.sync.dma_start(out=r[:], in_=res_rows[:, s, :])
+            sums.append(r)
+
+        g_words = []
+        g_scales = []
+        for e in range(2):
+            gs = tile("gs%d" % e, [P, J], U8)
+            nc.vector.tensor_copy(gs[:], xs[:].indirect(lists[e][:]))
+            queue = nc.scalar if e == 0 else nc.sync
+            for lo, n in ((0, 64), (64, 4), (96, 4)):
+                queue.dma_start(out=moved[e][lo : lo + n, :].bitcast(I32), in_=gs[lo + 4 : lo + 4 + n, :].bitcast(I32))
+            g_scales.append([gs, moved[e]])
+            ws = []
+            for a in range(PASSES):
+                g = tile("gw%d%d" % (e, a), [P, J], U16)
+                nc.vector.tensor_copy(g[:], xw[a][:].indirect(lists[e][:]))
+                ws.append(g)
+            g_words.append(ws)
+
+        wmp = tile("wmp", [P, M], I32)
+        nc.vector.tensor_copy(
+            out=wmp[:].rearrange("p (s m) -> p s m", s=PACK), in_=wm[:].rearrange("p (m s) -> p s m", s=PACK)
+        )
+        wmsp = tile("wmsp", [P, M], U8)
+        nc.vector.tensor_copy(
+            out=wmsp[:].rearrange("p (s m) -> p s m", s=PACK), in_=wms[:, 0, :].rearrange("p (m s) -> p s m", s=PACK)
+        )
+
+        w_ops = [
+            [wa[a][:].bitcast(FP8X4) for a in range(PASSES)],
+            [wb[:, a, :].bitcast(FP4X4) for a in range(PASSES)],
+        ]
+        w_scales = [was, wbs]
+        tags = [["m%d" % i for i in range(4)], ["t%d" % i for i in range(4)]]
+
+        pairs = [tile("h01", [P, 2, T], BF16), tile("h23", [P, 2, T], BF16)]
+        grouped = [tile("hg%d" % c, [P, CHUNK, PACK], BF16) for c in range(CHUNKS)]
+
+        for e in range(2):
+            accs = [bank("acc%d%d" % (e, jb), tags[e][jb], [P, N]) for jb in range(J // P)]
+            for a in range(PASSES):
+                for jb in range(J // P):
+                    cols = slice(jb * P, (jb + 1) * P)
+                    nc.tensor.matmul_mx(
+                        out=accs[jb][:],
+                        lhsT=g_words[e][a][:, cols].bitcast(FP4X4),
+                        lhsT_scale=g_scales[e][a][:, cols],
+                        rhs=w_ops[e][a],
+                        rhs_scale=w_scales[e][:, a, :],
+                        start=(a == 0),
+                        stop=(a == PASSES - 1),
+                    )
+            gated = []
+            for jb in range(J // P):
+                pt = tile("pt%d%d" % (e, jb), [P, PACK, P], F32)
+                nc.scalar.activation(
+                    out=pt[:], in_=accs[jb][:].rearrange("j (p s) -> j s p", s=PACK), func=COPY,
+                    scale=gates[e][:, jb : jb + 1],
+                )
+                gated.append(pt)
+            for s in range(PACK):
+                turned = bank("turn%d%d" % (e, s), tags[1 - e][s], [P, J])
+                for jb in range(J // P):
+                    nc.tensor.transpose(turned[:, jb * P : (jb + 1) * P], gated[jb][:, s, :], ident[:])
+                src = tile("src%d%d" % (e, s), [P, J], F32)
+                nc.scalar.copy(out=src[:], in_=turned[:])
+                win = windows[e][s % 2]
+                nc.vector.tensor_copy(win[:].indirect(lists[e][:]), src[:])
+                if e == 0:
+                    nc.gpsimd.tensor_tensor(out=sums[s][:], in0=win[:], in1=sums[s][:], op=ADD)
+                elif s < PACK - 1:
+                    nc.gpsimd.tensor_tensor(out=pairs[s // 2][:, s % 2, :], in0=win[:], in1=sums[s][:], op=ADD)
+                    if s == 1:
+                        for c in range(CHUNKS):
+                            cols = slice(c * CHUNK, (c + 1) * CHUNK)
+                            nc.scalar.activation(
+                                out=grouped[c][:, :, 0:2], in_=pairs[0][:, :, cols].rearrange("p e c -> p c e"), func=RELU
+                            )
+
+        last = windows[1][(PACK - 1) % 2]
+        y_tags = [("t0", "t1"), ("t2", "t3"), ("m0", "m1"), ("m2", "m3")]
+        out_rows = out_0.rearrange("(p s) t -> p s t", s=PACK)
+        out_words = out_1.rearrange("z p c r -> p (z c r)").bitcast(I32)
+        y_scales = tile("y_scales", [P, T], U8)
+        hq = []
+
+        def front(c):
+            cols = slice(c * CHUNK, (c + 1) * CHUNK)
+            src = pairs[1][:, :, cols].rearrange("p e c -> p c e")
+            if c in (1, 2):
+                nc.scalar.activation(out=grouped[c][:, :, 2:4], in_=src, func=RELU)
+            else:
+                nc.vector.tensor_scalar(out=grouped[c][:, :, 2:4], in0=src, scalar1=0.0, scalar2=None, op0=MAX)
+
+        def quant(c):
+            words = tile("hq%d" % c, [P, CHUNK], I32)
+            scales = tile("hs%d" % c, [P, CHUNK], U8)
+            nc.vector.quantize_mx(
+                out=words[:].bitcast(FP8X4), scales=scales[:], in_=grouped[c][:].rearrange("p c s -> p (c s)")
+            )
+            hq.append((words, scales))
+
+        def add(c):
+            cols = slice(c * CHUNK, (c + 1) * CHUNK)
+            nc.vector.tensor_tensor(out=pairs[1][:, 1, cols], in0=last[:, cols], in1=sums[PACK - 1][:, cols], op=ADD)
+
+        ys = []
+
+        def product(c):
+            cols = slice(c * CHUNK, (c + 1) * CHUNK)
+            words, scales = hq[c]
+            y = tile("y%d" % c, [P, PACK, CHUNK], F32)
+            for h in range(2):
+                acc = bank("yacc%d%d" % (c, h), y_tags[c][h], [P, 2, CHUNK])
+                for i in range(2):
+                    s = 2 * h + i
+                    nc.tensor.matmul_mx(
+                        out=acc[:, i, :],
+                        lhsT=wmp[:, s * P : (s + 1) * P].bitcast(FP8X4),
+                        lhsT_scale=wmsp[:, s * P : (s + 1) * P],
+                        rhs=words[:].bitcast(FP8X4),
+                        rhs_scale=scales[:],
+                        start=True,
+                        stop=True,
+                    )
+                nc.scalar.copy(out=y[:, 2 * h : 2 * h + 2, :], in_=acc[:])
+                nc.sync.dma_start(out=out_rows[:, 2 * h : 2 * h + 2, cols], in_=y[:, 2 * h : 2 * h + 2, :])
+            ys.append(y)
+
+        ybs = []
+
+        def round_y(c):
+            yb = tile("yb%d" % c, [P, CHUNK, PACK], BF16)
+            nc.vector.tensor_copy(out=yb[:], in_=ys[c][:].rearrange("p s c -> p c s"))
+            ybs.append(yb)
+
+        def planes(c):
+            cols = slice(c * CHUNK, (c + 1) * CHUNK)
+            words = tile("yw%d" % c, [P, CHUNK], I32)
+            nc.vector.quantize_mx(
+                out=words[:].bitcast(FP8X4), scales=y_scales[:, cols], in_=ybs[c][:].rearrange("p c s -> p (c s)")
+            )
+            nc.sync.dma_start(out=out_words[:, cols], in_=words[:])
+
+        add(0)
+        add(1)
+        front(0)
+        front(1)
+        add(2)
+        quant(0)
+        front(2)
+        add(3)
+        product(0)
+        quant(1)
+        front(3)
+        product(1)
+        quant(2)
+        product(2)
+        quant(3)
+        product(3)
+        round_y(0)
+        round_y(1)
+        planes(0)
+        round_y(2)
+        planes(1)
+        round_y(3)
+        planes(2)
+        planes(3)
+        for q in range(QUADS):
+            nc.sync.dma_start(
+                out=out_2[0, 4 * q : 4 * q + 4, :].bitcast(I32), in_=y_scales[32 * q : 32 * q + 4, :].bitcast(I32)
+            )

@@ -22,8 +22,12 @@ P = 128
 PACK = 4
 PASSES = 2
 QUADS = 4
-CHUNK = 256
-CHUNKS = T // CHUNK
+WIDTHS = (128, 256, 256, 256, 128)
+PSUM_ROUND = ()
+STARTS = tuple(sum(WIDTHS[:c]) for c in range(len(WIDTHS)))
+CHUNKS = len(WIDTHS)
+SCALAR_FRONT = (1, 2)
+EARLY = 768
 
 
 def tile_moe_experts_then_shared_layer_pl_kernel(
@@ -41,24 +45,24 @@ def tile_moe_experts_then_shared_layer_pl_kernel(
         def bank(name, tag, shape):
             return ps.tile(shape, F32, name=name, tag=tag)
 
-        def zeroed_plane(name, shape):
+        def zeroed_plane(name, shape, engine):
             plane = tile(name, shape, U8)
-            nc.vector.memset(plane[:].bitcast(I32), 0)
+            engine.memset(plane[:].bitcast(I32), 0)
             return plane
 
-        def load_weight_scales(plane, scales):
+        def load_weight_scales(plane, scales, queue):
             for q in range(QUADS):
-                nc.sync.dma_start(
+                queue.dma_start(
                     out=plane[32 * q : 32 * q + 4, :, :].bitcast(I32),
                     in_=scales[:, 4 * q : 4 * q + 4, :].rearrange("a r n -> r a n").bitcast(I32),
                 )
 
         lists = [tile("list_a", [P, J // 16], U16), tile("list_b", [P, J // 16], U16)]
-        xs = zeroed_plane("xs", [P, T])
-        was = zeroed_plane("was", [P, PASSES, N])
-        moved = [zeroed_plane("moved_a", [P, J]), zeroed_plane("moved_b", [P, J])]
-        wms = zeroed_plane("wms", [P, 1, M])
-        wbs = zeroed_plane("wbs", [P, PASSES, N])
+        xs = zeroed_plane("xs", [P, T], nc.gpsimd)
+        was = zeroed_plane("was", [P, PASSES, N], nc.gpsimd)
+        moved = [zeroed_plane("moved_a", [P, J], nc.vector), zeroed_plane("moved_b", [P, J], nc.vector)]
+        wms = zeroed_plane("wms", [P, 1, M], nc.vector)
+        wbs = zeroed_plane("wbs", [P, PASSES, N], nc.vector)
 
         ident = tile("ident", [P, P], F32)
         make_identity(nc, ident[:])
@@ -68,56 +72,55 @@ def tile_moe_experts_then_shared_layer_pl_kernel(
                 nc.gpsimd.memset(windows[e][b][:], 0.0)
 
         nc.sync.dma_start(lists[0][:], offs)
+        xw = [tile("xw%d" % a, [P, T], U16) for a in range(PASSES)]
+        wa = tile("wa", [P, PASSES, N], I32)
+        nc.sync.dma_start(out=xw[0][:].bitcast(I32), in_=xt_words[0].bitcast(I32))
         for q in range(QUADS):
             nc.sync.dma_start(
                 out=xs[32 * q : 32 * q + 8, :].bitcast(I32),
                 in_=xt_scales[:, 4 * q : 4 * q + 4, :].bitcast(I32),
             )
-        xw = []
-        for a in range(PASSES):
-            w = tile("xw%d" % a, [P, T], U16)
-            nc.sync.dma_start(out=w[:].bitcast(I32), in_=xt_words[a].bitcast(I32))
-            xw.append(w)
+        nc.sync.dma_start(out=xw[1][:].bitcast(I32), in_=xt_words[1].bitcast(I32))
+        nc.sync.dma_start(out=wa[:], in_=wa_words.rearrange("a p n t -> p a (n t)").bitcast(I32))
+        load_weight_scales(was, wa_scales, nc.sync)
         nc.sync.dma_start(lists[1][:], offs2)
-        load_weight_scales(was, wa_scales)
-        wa = []
-        for a in range(PASSES):
-            w = tile("wa%d" % a, [P, N], I32)
-            nc.sync.dma_start(out=w[:], in_=wa_words[a].rearrange("p n t -> p (n t)").bitcast(I32))
-            wa.append(w)
         gates = [tile("gate_a", [P, J // P], F32), tile("gate_b", [P, J // P], F32)]
         with nc.allow_non_contiguous_dma(reason="one gate to a partition"):
             nc.sync.dma_start(out=gates[0][:], in_=ga.rearrange("o (c p) -> p (o c)", p=P))
+
+        g_words = [[tile("gw%d%d" % (e, a), [P, J], U16) for a in range(PASSES)] for e in range(2)]
+        g_scales = [[tile("gs%d" % e, [P, J], U8), moved[e]] for e in range(2)]
+
+        def gather_words(e, a):
+            nc.vector.tensor_copy(g_words[e][a][:], xw[a][:].indirect(lists[e][:]))
+
+        def gather_scales(e):
+            gs = g_scales[e][0]
+            nc.vector.tensor_copy(gs[:], xs[:].indirect(lists[e][:]))
+            for lo, n in ((0, 64), (64, 4), (96, 4)):
+                nc.sync.dma_start(
+                    out=moved[e][lo : lo + n, :].bitcast(I32), in_=gs[lo + 4 : lo + 4 + n, :].bitcast(I32)
+                )
+
+        gather_words(0, 0)
+        gather_scales(0)
+        gather_words(0, 1)
         wm = tile("wm", [P, M], I32)
         nc.sync.dma_start(out=wm[:], in_=wm_words[0].rearrange("p n t -> p (n t)").bitcast(I32))
-        load_weight_scales(wms, wm_scales)
-        load_weight_scales(wbs, wb_scales)
+        load_weight_scales(wms, wm_scales, nc.sync)
+        gather_scales(1)
+        gather_words(1, 0)
+        gather_words(1, 1)
+        res_rows = res.rearrange("(p s) t -> p s t", s=PACK)
+        sums = [tile("res%d" % s, [P, T], F32) for s in range(PACK)]
+        nc.sync.dma_start(out=sums[0][:], in_=res_rows[:, 0, :])
+        load_weight_scales(wbs, wb_scales, nc.sync)
         wb = tile("wb", [P, PASSES, N // 2], I32)
         nc.sync.dma_start(out=wb[:], in_=wb_words.rearrange("a p n -> p a n").bitcast(I32))
         with nc.allow_non_contiguous_dma(reason="one gate to a partition"):
             nc.sync.dma_start(out=gates[1][:], in_=gb.rearrange("o (c p) -> p (o c)", p=P))
-        sums = []
-        res_rows = res.rearrange("(p s) t -> p s t", s=PACK)
-        for s in range(PACK):
-            r = tile("res%d" % s, [P, T], F32)
-            nc.sync.dma_start(out=r[:], in_=res_rows[:, s, :])
-            sums.append(r)
-
-        g_words = []
-        g_scales = []
-        for e in range(2):
-            gs = tile("gs%d" % e, [P, J], U8)
-            nc.vector.tensor_copy(gs[:], xs[:].indirect(lists[e][:]))
-            queue = nc.scalar if e == 0 else nc.sync
-            for lo, n in ((0, 64), (64, 4), (96, 4)):
-                queue.dma_start(out=moved[e][lo : lo + n, :].bitcast(I32), in_=gs[lo + 4 : lo + 4 + n, :].bitcast(I32))
-            g_scales.append([gs, moved[e]])
-            ws = []
-            for a in range(PASSES):
-                g = tile("gw%d%d" % (e, a), [P, J], U16)
-                nc.vector.tensor_copy(g[:], xw[a][:].indirect(lists[e][:]))
-                ws.append(g)
-            g_words.append(ws)
+        for s in range(1, PACK):
+            nc.sync.dma_start(out=sums[s][:], in_=res_rows[:, s, :])
 
         wmp = tile("wmp", [P, M], I32)
         nc.vector.tensor_copy(
@@ -129,19 +132,21 @@ def tile_moe_experts_then_shared_layer_pl_kernel(
         )
 
         w_ops = [
-            [wa[a][:].bitcast(FP8X4) for a in range(PASSES)],
+            [wa[:, a, :].bitcast(FP8X4) for a in range(PASSES)],
             [wb[:, a, :].bitcast(FP4X4) for a in range(PASSES)],
         ]
         w_scales = [was, wbs]
-        tags = [["m%d" % i for i in range(4)], ["t%d" % i for i in range(4)]]
 
         pairs = [tile("h01", [P, 2, T], BF16), tile("h23", [P, 2, T], BF16)]
-        grouped = [tile("hg%d" % c, [P, CHUNK, PACK], BF16) for c in range(CHUNKS)]
+        grouped = [tile("hg%d" % c, [P, WIDTHS[c], PACK], BF16) for c in range(CHUNKS)]
 
-        for e in range(2):
-            accs = [bank("acc%d%d" % (e, jb), tags[e][jb], [P, N]) for jb in range(J // P)]
+        srcs = [[tile("src%d%d" % (e, s), [P, J], F32) for s in range(PACK)] for e in range(2)]
+        acc_tags = [["m0", "m1", "m2", "m3"], ["t1", "t2", "t3", "t0"]]
+        blocks = J // P
+
+        def products(e, jbs):
             for a in range(PASSES):
-                for jb in range(J // P):
+                for jb in jbs:
                     cols = slice(jb * P, (jb + 1) * P)
                     nc.tensor.matmul_mx(
                         out=accs[jb][:],
@@ -152,70 +157,117 @@ def tile_moe_experts_then_shared_layer_pl_kernel(
                         start=(a == 0),
                         stop=(a == PASSES - 1),
                     )
-            gated = []
-            for jb in range(J // P):
-                pt = tile("pt%d%d" % (e, jb), [P, PACK, P], F32)
+
+        def gate(e, jbs, s0, s1):
+            for jb in jbs:
                 nc.scalar.activation(
-                    out=pt[:], in_=accs[jb][:].rearrange("j (p s) -> j s p", s=PACK), func=COPY,
+                    out=gated[jb][:, s0:s1, :],
+                    in_=accs[jb][:].rearrange("j (p s) -> j s p", s=PACK)[:, s0:s1, :],
+                    func=COPY,
                     scale=gates[e][:, jb : jb + 1],
                 )
-                gated.append(pt)
-            for s in range(PACK):
-                turned = bank("turn%d%d" % (e, s), tags[1 - e][s], [P, J])
-                for jb in range(J // P):
-                    nc.tensor.transpose(turned[:, jb * P : (jb + 1) * P], gated[jb][:, s, :], ident[:])
-                src = tile("src%d%d" % (e, s), [P, J], F32)
-                nc.scalar.copy(out=src[:], in_=turned[:])
-                win = windows[e][s % 2]
-                nc.vector.tensor_copy(win[:].indirect(lists[e][:]), src[:])
-                if e == 0:
-                    nc.gpsimd.tensor_tensor(out=sums[s][:], in0=win[:], in1=sums[s][:], op=ADD)
-                elif s < PACK - 1:
-                    nc.gpsimd.tensor_tensor(out=pairs[s // 2][:, s % 2, :], in0=win[:], in1=sums[s][:], op=ADD)
-                    if s == 1:
-                        for c in range(CHUNKS):
-                            cols = slice(c * CHUNK, (c + 1) * CHUNK)
-                            nc.scalar.activation(
-                                out=grouped[c][:, :, 0:2], in_=pairs[0][:, :, cols].rearrange("p e c -> p c e"), func=RELU
-                            )
 
-        last = windows[1][(PACK - 1) % 2]
-        y_tags = [("t0", "t1"), ("t2", "t3"), ("m0", "m1"), ("m2", "m3")]
+        def turn(e, s, jbs, tag):
+            turned = bank("turn%d%d%d" % (e, s, jbs[0]), tag, [P, len(jbs) * P])
+            for i, jb in enumerate(jbs):
+                nc.tensor.transpose(turned[:, i * P : (i + 1) * P], gated[jb][:, s, :], ident[:])
+            nc.scalar.copy(out=srcs[e][s][:, jbs[0] * P : (jbs[-1] + 1) * P], in_=turned[:])
+
+        accs = [bank("acc0%d" % jb, acc_tags[0][jb], [P, N]) for jb in range(blocks)]
+        gated = [tile("pt0%d" % jb, [P, PACK, P], F32) for jb in range(blocks)]
+        for half, tag in (((0, 1), "t0"), ((2, 3), "t1")):
+            products(0, half)
+            gate(0, half, 0, 1)
+            turn(0, 0, half, tag)
+        gate(0, range(blocks), 1, PACK)
+        for s, tag in ((1, "t2"), (2, "t3"), (3, "t0")):
+            turn(0, s, range(blocks), tag)
+        accs = [bank("acc1%d" % jb, acc_tags[1][jb], [P, N]) for jb in range(blocks)]
+        gated = [tile("pt1%d" % jb, [P, PACK, P], F32) for jb in range(blocks)]
+        products(1, range(blocks))
+        gate(1, range(blocks), 0, PACK)
+        for s in range(PACK):
+            turn(1, s, range(blocks), acc_tags[0][s])
+
+        def scatter(e, s):
+            nc.vector.tensor_copy(windows[e][s % 2][:].indirect(lists[e][:]), srcs[e][s][:])
+
+        def onto_res(e, s, cols):
+            nc.gpsimd.tensor_tensor(out=sums[s][:, cols], in0=windows[e][s % 2][:, cols], in1=sums[s][:, cols], op=ADD)
+
+        def finish(e, s, cols):
+            nc.gpsimd.tensor_tensor(
+                out=pairs[s // 2][:, s % 2, cols], in0=windows[e][s % 2][:, cols], in1=sums[s][:, cols], op=ADD
+            )
+
+        every, early, late = slice(0, T), slice(0, EARLY), slice(EARLY, T)
+        for h in range(2):
+            nc.vector.tensor_copy(
+                windows[0][0][:].indirect(lists[0][:, 16 * h : 16 * h + 16]), srcs[0][0][:, 256 * h : 256 * h + 256]
+            )
+        onto_res(0, 0, every)
+        scatter(0, 1)
+        onto_res(0, 1, early)
+        scatter(0, 2)
+        onto_res(0, 2, every)
+        scatter(1, 0)
+        finish(1, 0, every)
+        scatter(1, 1)
+        finish(1, 1, early)
+        onto_res(1, 1, late)
+        finish(0, 1, late)
+        for c in range(CHUNKS):
+            cols = slice(STARTS[c], STARTS[c] + WIDTHS[c])
+            nc.scalar.activation(
+                out=grouped[c][:, :, 0:2], in_=pairs[0][:, :, cols].rearrange("p e c -> p c e"), func=RELU
+            )
+        scatter(1, 2)
+        finish(1, 2, every)
+        scatter(1, 3)
+        onto_res(1, 3, every)
+        scatter(0, 3)
+
+        last = windows[0][(PACK - 1) % 2]
+        y_tags = ["t0", "t1", "t2", "t3", "m0", "m1", "m2", "m3"]
+        used = []
         out_rows = out_0.rearrange("(p s) t -> p s t", s=PACK)
         out_words = out_1.rearrange("z p c r -> p (z c r)").bitcast(I32)
         y_scales = tile("y_scales", [P, T], U8)
         hq = []
 
         def front(c):
-            cols = slice(c * CHUNK, (c + 1) * CHUNK)
+            cols = slice(STARTS[c], STARTS[c] + WIDTHS[c])
             src = pairs[1][:, :, cols].rearrange("p e c -> p c e")
-            if c in (1, 2):
+            if c in SCALAR_FRONT:
                 nc.scalar.activation(out=grouped[c][:, :, 2:4], in_=src, func=RELU)
             else:
                 nc.vector.tensor_scalar(out=grouped[c][:, :, 2:4], in0=src, scalar1=0.0, scalar2=None, op0=MAX)
 
         def quant(c):
-            words = tile("hq%d" % c, [P, CHUNK], I32)
-            scales = tile("hs%d" % c, [P, CHUNK], U8)
+            words = tile("hq%d" % c, [P, WIDTHS[c]], I32)
+            scales = tile("hs%d" % c, [P, WIDTHS[c]], U8)
             nc.vector.quantize_mx(
                 out=words[:].bitcast(FP8X4), scales=scales[:], in_=grouped[c][:].rearrange("p c s -> p (c s)")
             )
             hq.append((words, scales))
 
         def add(c):
-            cols = slice(c * CHUNK, (c + 1) * CHUNK)
+            cols = slice(STARTS[c], STARTS[c] + WIDTHS[c])
             nc.vector.tensor_tensor(out=pairs[1][:, 1, cols], in0=last[:, cols], in1=sums[PACK - 1][:, cols], op=ADD)
 
         ys = []
+        ybs = {}
 
         def product(c):
-            cols = slice(c * CHUNK, (c + 1) * CHUNK)
+            cols = slice(STARTS[c], STARTS[c] + WIDTHS[c])
             words, scales = hq[c]
-            y = tile("y%d" % c, [P, PACK, CHUNK], F32)
-            for h in range(2):
-                acc = bank("yacc%d%d" % (c, h), y_tags[c][h], [P, 2, CHUNK])
-                for i in range(2):
-                    s = 2 * h + i
+            y = tile("y%d" % c, [P, PACK, WIDTHS[c]], F32)
+            per_bank = 512 // WIDTHS[c]
+            for s0 in range(0, PACK, per_bank):
+                acc = bank("yacc%d%d" % (c, s0), y_tags[len(used)], [P, per_bank, WIDTHS[c]])
+                used.append(c)
+                for i in range(per_bank):
+                    s = s0 + i
                     nc.tensor.matmul_mx(
                         out=acc[:, i, :],
                         lhsT=wmp[:, s * P : (s + 1) * P].bitcast(FP8X4),
@@ -225,20 +277,23 @@ def tile_moe_experts_then_shared_layer_pl_kernel(
                         start=True,
                         stop=True,
                     )
-                nc.scalar.copy(out=y[:, 2 * h : 2 * h + 2, :], in_=acc[:])
-                nc.sync.dma_start(out=out_rows[:, 2 * h : 2 * h + 2, cols], in_=y[:, 2 * h : 2 * h + 2, :])
+                if c in PSUM_ROUND:
+                    yb = tile("yb%d" % c, [P, WIDTHS[c], PACK], BF16)
+                    nc.vector.tensor_copy(out=yb[:], in_=acc[:].rearrange("p s c -> p c s"))
+                    ybs[c] = yb
+                nc.scalar.copy(out=y[:, s0 : s0 + per_bank, :], in_=acc[:])
+                nc.sync.dma_start(out=out_rows[:, s0 : s0 + per_bank, cols], in_=y[:, s0 : s0 + per_bank, :])
             ys.append(y)
 
-        ybs = []
 
         def round_y(c):
-            yb = tile("yb%d" % c, [P, CHUNK, PACK], BF16)
+            yb = tile("yb%d" % c, [P, WIDTHS[c], PACK], BF16)
             nc.vector.tensor_copy(out=yb[:], in_=ys[c][:].rearrange("p s c -> p c s"))
-            ybs.append(yb)
+            ybs[c] = yb
 
         def planes(c):
-            cols = slice(c * CHUNK, (c + 1) * CHUNK)
-            words = tile("yw%d" % c, [P, CHUNK], I32)
+            cols = slice(STARTS[c], STARTS[c] + WIDTHS[c])
+            words = tile("yw%d" % c, [P, WIDTHS[c]], I32)
             nc.vector.quantize_mx(
                 out=words[:].bitcast(FP8X4), scales=y_scales[:, cols], in_=ybs[c][:].rearrange("p c s -> p (c s)")
             )
@@ -250,25 +305,31 @@ def tile_moe_experts_then_shared_layer_pl_kernel(
         front(1)
         add(2)
         quant(0)
+        product(0)
         front(2)
         add(3)
-        product(0)
         quant(1)
-        front(3)
         product(1)
+        add(4)
+        front(3)
         quant(2)
         product(2)
+        front(4)
         quant(3)
         product(3)
         round_y(0)
+        quant(4)
+        product(4)
         round_y(1)
         planes(0)
         round_y(2)
         planes(1)
         round_y(3)
         planes(2)
+        round_y(4)
         planes(3)
+        planes(4)
         for q in range(QUADS):
-            nc.sync.dma_start(
+            (nc.scalar if q % 2 else nc.sync).dma_start(
                 out=out_2[0, 4 * q : 4 * q + 4, :].bitcast(I32), in_=y_scales[32 * q : 32 * q + 4, :].bitcast(I32)
             )

@@ -23,7 +23,7 @@ PACK = 4
 PASSES = 2
 QUADS = 4
 WIDTHS = (128, 256, 256, 256, 128)
-PSUM_ROUND = ()
+PSUM_ROUND = (4,)
 STARTS = tuple(sum(WIDTHS[:c]) for c in range(len(WIDTHS)))
 CHUNKS = len(WIDTHS)
 SCALAR_FRONT = (1, 2)
@@ -124,7 +124,7 @@ def tile_moe_experts_then_shared_layer_pl_kernel(
 
         wmp = tile("wmp", [P, M], I32)
         nc.vector.tensor_copy(
-            out=wmp[:].rearrange("p (s m) -> p s m", s=PACK), in_=wm[:].rearrange("p (m s) -> p s m", s=PACK)
+            out=wmp[:].rearrange("p (s m) -> p m s", s=PACK), in_=wm[:].rearrange("p (m s) -> p m s", s=PACK)
         )
         wmsp = tile("wmsp", [P, M], U8)
         nc.vector.tensor_copy(
@@ -138,7 +138,9 @@ def tile_moe_experts_then_shared_layer_pl_kernel(
         w_scales = [was, wbs]
 
         pairs = [tile("h01", [P, 2, T], BF16), tile("h23", [P, 2, T], BF16)]
-        grouped = [tile("hg%d" % c, [P, WIDTHS[c], PACK], BF16) for c in range(CHUNKS)]
+        grouped = [tile("hg%d" % c, [P, WIDTHS[c], PACK], BF16)[:] for c in range(3)]
+        tail_group = tile("hg_tail", [P, WIDTHS[3] + WIDTHS[4], PACK], BF16)
+        grouped = grouped + [tail_group[:, 0 : WIDTHS[3], :], tail_group[:, WIDTHS[3] :, :]]
 
         srcs = [[tile("src%d%d" % (e, s), [P, J], F32) for s in range(PACK)] for e in range(2)]
         acc_tags = [["m0", "m1", "m2", "m3"], ["t1", "t2", "t3", "t0"]]
@@ -224,7 +226,21 @@ def tile_moe_experts_then_shared_layer_pl_kernel(
         scatter(1, 2)
         finish(1, 2, every)
         scatter(1, 3)
-        onto_res(1, 3, every)
+        warm = bank("warm", "m3", [P, N])
+        for lo, hi, count in ((0, 0, 1), (0, 512, 2), (512, T, 2)):
+            if hi > lo:
+                onto_res(1, 3, slice(lo, hi))
+            nc.tensor.transpose(warm[:, 0:P], sums[3][:, hi - P : hi] if hi > lo else windows[1][1][:, 0:P], ident[:])
+            for i in range(count):
+                nc.tensor.matmul_mx(
+                    out=warm[:],
+                    lhsT=g_words[0][0][:, 0:P].bitcast(FP4X4),
+                    lhsT_scale=g_scales[0][0][:, 0:P],
+                    rhs=w_ops[0][0],
+                    rhs_scale=w_scales[0][:, 0, :],
+                    start=True,
+                    stop=True,
+                )
         scatter(0, 3)
 
         last = windows[0][(PACK - 1) % 2]
@@ -233,6 +249,7 @@ def tile_moe_experts_then_shared_layer_pl_kernel(
         out_rows = out_0.rearrange("(p s) t -> p s t", s=PACK)
         out_words = out_1.rearrange("z p c r -> p (z c r)").bitcast(I32)
         y_scales = tile("y_scales", [P, T], U8)
+        y_words = tile("y_words", [P, T], I32)
         hq = []
 
         def front(c):
@@ -240,6 +257,9 @@ def tile_moe_experts_then_shared_layer_pl_kernel(
             src = pairs[1][:, :, cols].rearrange("p e c -> p c e")
             if c in SCALAR_FRONT:
                 nc.scalar.activation(out=grouped[c][:, :, 2:4], in_=src, func=RELU)
+            elif c == 3:
+                src = pairs[1][:, :, STARTS[3] : T].rearrange("p e c -> p c e")
+                nc.vector.tensor_scalar(out=tail_group[:, :, 2:4], in0=src, scalar1=0.0, scalar2=None, op0=MAX)
             else:
                 nc.vector.tensor_scalar(out=grouped[c][:, :, 2:4], in0=src, scalar1=0.0, scalar2=None, op0=MAX)
 
@@ -247,12 +267,12 @@ def tile_moe_experts_then_shared_layer_pl_kernel(
             words = tile("hq%d" % c, [P, WIDTHS[c]], I32)
             scales = tile("hs%d" % c, [P, WIDTHS[c]], U8)
             nc.vector.quantize_mx(
-                out=words[:].bitcast(FP8X4), scales=scales[:], in_=grouped[c][:].rearrange("p c s -> p (c s)")
+                out=words[:].bitcast(FP8X4), scales=scales[:], in_=grouped[c].rearrange("p c s -> p (c s)")
             )
             hq.append((words, scales))
 
-        def add(c):
-            cols = slice(STARTS[c], STARTS[c] + WIDTHS[c])
+        def add(lo, hi):
+            cols = slice(lo, hi)
             nc.vector.tensor_tensor(out=pairs[1][:, 1, cols], in0=last[:, cols], in1=sums[PACK - 1][:, cols], op=ADD)
 
         ys = []
@@ -279,56 +299,64 @@ def tile_moe_experts_then_shared_layer_pl_kernel(
                     )
                 if c in PSUM_ROUND:
                     yb = tile("yb%d" % c, [P, WIDTHS[c], PACK], BF16)
-                    nc.vector.tensor_copy(out=yb[:], in_=acc[:].rearrange("p s c -> p c s"))
+                    nc.scalar.copy(out=yb[:], in_=acc[:].rearrange("p s c -> p c s"))
                     ybs[c] = yb
                 nc.scalar.copy(out=y[:, s0 : s0 + per_bank, :], in_=acc[:])
-                nc.sync.dma_start(out=out_rows[:, s0 : s0 + per_bank, cols], in_=y[:, s0 : s0 + per_bank, :])
+                if c != 3:
+                    nc.sync.dma_start(out=out_rows[:, s0 : s0 + per_bank, cols], in_=y[:, s0 : s0 + per_bank, :])
+            if c == 3:
+                nc.sync.dma_start(out=out_rows[:, :, cols], in_=y[:])
             ys.append(y)
 
 
         def round_y(c):
             yb = tile("yb%d" % c, [P, WIDTHS[c], PACK], BF16)
-            nc.vector.tensor_copy(out=yb[:], in_=ys[c][:].rearrange("p s c -> p c s"))
+            nc.vector.tensor_copy(
+                out=yb[:].rearrange("p (c i) s -> p c s i", i=4), in_=ys[c][:].rearrange("p s (c i) -> p c s i", i=4)
+            )
             ybs[c] = yb
 
         def planes(c):
             cols = slice(STARTS[c], STARTS[c] + WIDTHS[c])
-            words = tile("yw%d" % c, [P, WIDTHS[c]], I32)
             nc.vector.quantize_mx(
-                out=words[:].bitcast(FP8X4), scales=y_scales[:, cols], in_=ybs[c][:].rearrange("p c s -> p (c s)")
+                out=y_words[:, cols].bitcast(FP8X4), scales=y_scales[:, cols], in_=ybs[c][:].rearrange("p c s -> p (c s)")
             )
-            nc.sync.dma_start(out=out_words[:, cols], in_=words[:])
 
-        add(0)
-        add(1)
+        def store_words(c0, c1):
+            cols = slice(STARTS[c0], STARTS[c1] + WIDTHS[c1])
+            nc.sync.dma_start(out=out_words[:, cols], in_=y_words[:, cols])
+
+        add(0, 128)
+        add(128, 256)
         front(0)
+        add(256, 384)
         front(1)
-        add(2)
         quant(0)
         product(0)
+        add(384, 640)
         front(2)
-        add(3)
+        add(640, 1024)
         quant(1)
         product(1)
-        add(4)
         front(3)
         quant(2)
         product(2)
-        front(4)
         quant(3)
         product(3)
-        round_y(0)
         quant(4)
         product(4)
+        round_y(0)
         round_y(1)
         planes(0)
         round_y(2)
         planes(1)
+        store_words(0, 1)
         round_y(3)
         planes(2)
-        round_y(4)
-        planes(3)
+        store_words(2, 2)
         planes(4)
+        planes(3)
+        store_words(3, 4)
         for q in range(QUADS):
             (nc.scalar if q % 2 else nc.sync).dma_start(
                 out=out_2[0, 4 * q : 4 * q + 4, :].bitcast(I32), in_=y_scales[32 * q : 32 * q + 4, :].bitcast(I32)

@@ -19,15 +19,19 @@ COPY = mybir.ActivationFunctionType.Copy
 RELU = mybir.ActivationFunctionType.Relu
 
 P = 128
-PACK = 4
-PASSES = 2
+SLOTS = 4
+PASSES = K // (P * SLOTS)
 QUADS = 4
+BLOCKS = J // P
+PER_COLUMN = 16
+BANK = 512
+LINE = 4
+A, B = 0, 1
+
 WIDTHS = (128, 256, 256, 256, 128)
-PSUM_ROUND = (4,)
 STARTS = tuple(sum(WIDTHS[:c]) for c in range(len(WIDTHS)))
-CHUNKS = len(WIDTHS)
-SCALAR_FRONT = (1, 2)
-EARLY = 768
+LAST = len(WIDTHS) - 1
+A_FIRST = 768
 
 
 def tile_moe_experts_then_shared_layer_pl_kernel(
@@ -42,322 +46,307 @@ def tile_moe_experts_then_shared_layer_pl_kernel(
         def tile(name, shape, dtype):
             return sb.tile(shape, dtype, name=name, align_bytes=64)
 
-        def bank(name, tag, shape):
-            return ps.tile(shape, F32, name=name, tag=tag)
+        def bank(name, number, shape):
+            return ps.tile(shape, F32, name=name, tag="bank%d" % number)
+
+        def chunk(c):
+            return slice(STARTS[c], STARTS[c] + WIDTHS[c])
 
         def zeroed_plane(name, shape, engine):
             plane = tile(name, shape, U8)
             engine.memset(plane[:].bitcast(I32), 0)
             return plane
 
-        def load_weight_scales(plane, scales, queue):
+        def load_weight_scales(plane, scales):
             for q in range(QUADS):
-                queue.dma_start(
+                nc.sync.dma_start(
                     out=plane[32 * q : 32 * q + 4, :, :].bitcast(I32),
                     in_=scales[:, 4 * q : 4 * q + 4, :].rearrange("a r n -> r a n").bitcast(I32),
                 )
 
-        lists = [tile("list_a", [P, J // 16], U16), tile("list_b", [P, J // 16], U16)]
-        xs = zeroed_plane("xs", [P, T], nc.gpsimd)
-        was = zeroed_plane("was", [P, PASSES, N], nc.gpsimd)
+        def load_gate(name, gate_row):
+            gate_tile = tile(name, [P, BLOCKS], F32)
+            with nc.allow_non_contiguous_dma(reason="one gate to a partition"):
+                nc.sync.dma_start(out=gate_tile[:], in_=gate_row.rearrange("o (b p) -> p (o b)", p=P))
+            return gate_tile
+
+        lists = [tile("list_a", [P, J // PER_COLUMN], U16), tile("list_b", [P, J // PER_COLUMN], U16)]
+        x_scales = zeroed_plane("x_scales", [P, T], nc.gpsimd)
+        wa_plane = zeroed_plane("wa_plane", [P, PASSES, N], nc.gpsimd)
         moved = [zeroed_plane("moved_a", [P, J], nc.vector), zeroed_plane("moved_b", [P, J], nc.vector)]
-        wms = zeroed_plane("wms", [P, 1, M], nc.vector)
-        wbs = zeroed_plane("wbs", [P, PASSES, N], nc.vector)
+        wm_plane = zeroed_plane("wm_plane", [P, 1, M], nc.vector)
+        wb_plane = zeroed_plane("wb_plane", [P, PASSES, N], nc.vector)
 
         ident = tile("ident", [P, P], F32)
         make_identity(nc, ident[:])
-        windows = [[tile("win%d%d" % (e, b), [P, T], F32) for b in range(2)] for e in range(2)]
-        for e in range(2):
-            for b in range(2):
-                nc.gpsimd.memset(windows[e][b][:], 0.0)
+        windows = [[tile("window%d%d" % (e, i), [P, T], F32) for i in range(2)] for e in (A, B)]
+        for e in (A, B):
+            for window in windows[e]:
+                nc.gpsimd.memset(window[:], 0.0)
 
-        nc.sync.dma_start(lists[0][:], offs)
-        xw = [tile("xw%d" % a, [P, T], U16) for a in range(PASSES)]
+        x_words = [tile("x_words%d" % a, [P, T], U16) for a in range(PASSES)]
         wa = tile("wa", [P, PASSES, N], I32)
-        nc.sync.dma_start(out=xw[0][:].bitcast(I32), in_=xt_words[0].bitcast(I32))
+        nc.sync.dma_start(lists[A][:], offs)
+        nc.sync.dma_start(out=x_words[0][:].bitcast(I32), in_=xt_words[0].bitcast(I32))
         for q in range(QUADS):
             nc.sync.dma_start(
-                out=xs[32 * q : 32 * q + 8, :].bitcast(I32),
+                out=x_scales[32 * q : 32 * q + 4 * PASSES, :].bitcast(I32),
                 in_=xt_scales[:, 4 * q : 4 * q + 4, :].bitcast(I32),
             )
-        nc.sync.dma_start(out=xw[1][:].bitcast(I32), in_=xt_words[1].bitcast(I32))
-        nc.sync.dma_start(out=wa[:], in_=wa_words.rearrange("a p n t -> p a (n t)").bitcast(I32))
-        load_weight_scales(was, wa_scales, nc.sync)
-        nc.sync.dma_start(lists[1][:], offs2)
-        gates = [tile("gate_a", [P, J // P], F32), tile("gate_b", [P, J // P], F32)]
-        with nc.allow_non_contiguous_dma(reason="one gate to a partition"):
-            nc.sync.dma_start(out=gates[0][:], in_=ga.rearrange("o (c p) -> p (o c)", p=P))
+        nc.sync.dma_start(out=x_words[1][:].bitcast(I32), in_=xt_words[1].bitcast(I32))
+        nc.sync.dma_start(out=wa[:], in_=wa_words.rearrange("a p n r -> p a (n r)").bitcast(I32))
+        load_weight_scales(wa_plane, wa_scales)
+        nc.sync.dma_start(lists[B][:], offs2)
+        gates = [load_gate("gate_a", ga)]
 
-        g_words = [[tile("gw%d%d" % (e, a), [P, J], U16) for a in range(PASSES)] for e in range(2)]
-        g_scales = [[tile("gs%d" % e, [P, J], U8), moved[e]] for e in range(2)]
+        picked_words = [[tile("picked%d%d" % (e, a), [P, J], U16) for a in range(PASSES)] for e in (A, B)]
+        picked_planes = [[tile("picked_scales%d" % e, [P, J], U8), moved[e]] for e in (A, B)]
 
         def gather_words(e, a):
-            nc.vector.tensor_copy(g_words[e][a][:], xw[a][:].indirect(lists[e][:]))
+            nc.vector.tensor_copy(picked_words[e][a][:], x_words[a][:].indirect(lists[e][:]))
 
         def gather_scales(e):
-            gs = g_scales[e][0]
-            nc.vector.tensor_copy(gs[:], xs[:].indirect(lists[e][:]))
-            for lo, n in ((0, 64), (64, 4), (96, 4)):
+            both = picked_planes[e][0]
+            nc.vector.tensor_copy(both[:], x_scales[:].indirect(lists[e][:]))
+            for first, rows in ((0, 64), (64, 4), (96, 4)):
                 nc.sync.dma_start(
-                    out=moved[e][lo : lo + n, :].bitcast(I32), in_=gs[lo + 4 : lo + 4 + n, :].bitcast(I32)
+                    out=moved[e][first : first + rows, :].bitcast(I32),
+                    in_=both[first + 4 : first + 4 + rows, :].bitcast(I32),
                 )
 
-        gather_words(0, 0)
-        gather_scales(0)
-        gather_words(0, 1)
+        gather_words(A, 0)
+        gather_scales(A)
+        gather_words(A, 1)
         wm = tile("wm", [P, M], I32)
-        nc.sync.dma_start(out=wm[:], in_=wm_words[0].rearrange("p n t -> p (n t)").bitcast(I32))
-        load_weight_scales(wms, wm_scales, nc.sync)
-        gather_scales(1)
-        gather_words(1, 0)
-        gather_words(1, 1)
-        res_rows = res.rearrange("(p s) t -> p s t", s=PACK)
-        sums = [tile("res%d" % s, [P, T], F32) for s in range(PACK)]
-        nc.sync.dma_start(out=sums[0][:], in_=res_rows[:, 0, :])
-        load_weight_scales(wbs, wb_scales, nc.sync)
+        nc.sync.dma_start(out=wm[:], in_=wm_words[0].rearrange("p m r -> p (m r)").bitcast(I32))
+        load_weight_scales(wm_plane, wm_scales)
+        gather_scales(B)
+        gather_words(B, 0)
+        gather_words(B, 1)
+        load_weight_scales(wb_plane, wb_scales)
         wb = tile("wb", [P, PASSES, N // 2], I32)
         nc.sync.dma_start(out=wb[:], in_=wb_words.rearrange("a p n -> p a n").bitcast(I32))
-        with nc.allow_non_contiguous_dma(reason="one gate to a partition"):
-            nc.sync.dma_start(out=gates[1][:], in_=gb.rearrange("o (c p) -> p (o c)", p=P))
-        for s in range(1, PACK):
-            nc.sync.dma_start(out=sums[s][:], in_=res_rows[:, s, :])
+        res_slots = res.rearrange("(p s) t -> p s t", s=SLOTS)
+        sums = [tile("sum%d" % s, [P, T], F32) for s in range(SLOTS)]
+        nc.sync.dma_start(out=sums[0][:], in_=res_slots[:, 0, :])
+        gates.append(load_gate("gate_b", gb))
+        for s in range(1, SLOTS):
+            nc.sync.dma_start(out=sums[s][:], in_=res_slots[:, s, :])
 
-        wmp = tile("wmp", [P, M], I32)
+        wm_sorted = tile("wm_sorted", [P, M], I32)
         nc.vector.tensor_copy(
-            out=wmp[:].rearrange("p (s m) -> p m s", s=PACK), in_=wm[:].rearrange("p (m s) -> p m s", s=PACK)
+            out=wm_sorted[:].rearrange("p (s i) -> p i s", s=SLOTS), in_=wm[:].rearrange("p (i s) -> p i s", s=SLOTS)
         )
-        wmsp = tile("wmsp", [P, M], U8)
+        wm_plane_sorted = tile("wm_plane_sorted", [P, M], U8)
         nc.vector.tensor_copy(
-            out=wmsp[:].rearrange("p (s m) -> p s m", s=PACK), in_=wms[:, 0, :].rearrange("p (m s) -> p s m", s=PACK)
+            out=wm_plane_sorted[:].rearrange("p (s i) -> p s i", s=SLOTS),
+            in_=wm_plane[:, 0, :].rearrange("p (i s) -> p s i", s=SLOTS),
         )
 
-        w_ops = [
+        w_words = [
             [wa[:, a, :].bitcast(FP8X4) for a in range(PASSES)],
             [wb[:, a, :].bitcast(FP4X4) for a in range(PASSES)],
         ]
-        w_scales = [was, wbs]
+        w_planes = [wa_plane, wb_plane]
+        h_pairs = [tile("h_slots01", [P, 2, T], BF16), tile("h_slots23", [P, 2, T], BF16)]
+        h_grouped = [tile("h_grouped%d" % c, [P, WIDTHS[c], SLOTS], BF16)[:] for c in range(LAST - 1)]
+        h_grouped_end = tile("h_grouped_end", [P, WIDTHS[LAST - 1] + WIDTHS[LAST], SLOTS], BF16)
+        h_grouped.append(h_grouped_end[:, 0 : WIDTHS[LAST - 1], :])
+        h_grouped.append(h_grouped_end[:, WIDTHS[LAST - 1] :, :])
+        gated_slots = [[tile("gated%d%d" % (e, s), [P, J], F32) for s in range(SLOTS)] for e in (A, B)]
 
-        pairs = [tile("h01", [P, 2, T], BF16), tile("h23", [P, 2, T], BF16)]
-        grouped = [tile("hg%d" % c, [P, WIDTHS[c], PACK], BF16)[:] for c in range(3)]
-        tail_group = tile("hg_tail", [P, WIDTHS[3] + WIDTHS[4], PACK], BF16)
-        grouped = grouped + [tail_group[:, 0 : WIDTHS[3], :], tail_group[:, WIDTHS[3] :, :]]
-
-        srcs = [[tile("src%d%d" % (e, s), [P, J], F32) for s in range(PACK)] for e in range(2)]
-        acc_tags = [["m0", "m1", "m2", "m3"], ["t1", "t2", "t3", "t0"]]
-        blocks = J // P
-
-        def products(e, jbs):
+        def expert_products(e, blocks, accs):
             for a in range(PASSES):
-                for jb in jbs:
-                    cols = slice(jb * P, (jb + 1) * P)
+                for b in blocks:
+                    tokens = slice(b * P, (b + 1) * P)
                     nc.tensor.matmul_mx(
-                        out=accs[jb][:],
-                        lhsT=g_words[e][a][:, cols].bitcast(FP4X4),
-                        lhsT_scale=g_scales[e][a][:, cols],
-                        rhs=w_ops[e][a],
-                        rhs_scale=w_scales[e][:, a, :],
+                        out=accs[b][:],
+                        lhsT=picked_words[e][a][:, tokens].bitcast(FP4X4),
+                        lhsT_scale=picked_planes[e][a][:, tokens],
+                        rhs=w_words[e][a],
+                        rhs_scale=w_planes[e][:, a, :],
                         start=(a == 0),
                         stop=(a == PASSES - 1),
                     )
 
-        def gate(e, jbs, s0, s1):
-            for jb in jbs:
+        def gate(e, blocks, accs, by_token, s0, s1):
+            for b in blocks:
                 nc.scalar.activation(
-                    out=gated[jb][:, s0:s1, :],
-                    in_=accs[jb][:].rearrange("j (p s) -> j s p", s=PACK)[:, s0:s1, :],
+                    out=by_token[b][:, s0:s1, :],
+                    in_=accs[b][:].rearrange("j (i s) -> j s i", s=SLOTS)[:, s0:s1, :],
                     func=COPY,
-                    scale=gates[e][:, jb : jb + 1],
+                    scale=gates[e][:, b : b + 1],
                 )
 
-        def turn(e, s, jbs, tag):
-            turned = bank("turn%d%d%d" % (e, s, jbs[0]), tag, [P, len(jbs) * P])
-            for i, jb in enumerate(jbs):
-                nc.tensor.transpose(turned[:, i * P : (i + 1) * P], gated[jb][:, s, :], ident[:])
-            nc.scalar.copy(out=srcs[e][s][:, jbs[0] * P : (jbs[-1] + 1) * P], in_=turned[:])
+        def turn(e, s, blocks, by_token, number):
+            turned = bank("turned%d%d%d" % (e, s, blocks[0]), number, [P, len(blocks) * P])
+            for i, b in enumerate(blocks):
+                nc.tensor.transpose(turned[:, i * P : (i + 1) * P], by_token[b][:, s, :], ident[:])
+            nc.scalar.copy(out=gated_slots[e][s][:, blocks[0] * P : (blocks[-1] + 1) * P], in_=turned[:])
 
-        accs = [bank("acc0%d" % jb, acc_tags[0][jb], [P, N]) for jb in range(blocks)]
-        gated = [tile("pt0%d" % jb, [P, PACK, P], F32) for jb in range(blocks)]
-        for half, tag in (((0, 1), "t0"), ((2, 3), "t1")):
-            products(0, half)
-            gate(0, half, 0, 1)
-            turn(0, 0, half, tag)
-        gate(0, range(blocks), 1, PACK)
-        for s, tag in ((1, "t2"), (2, "t3"), (3, "t0")):
-            turn(0, s, range(blocks), tag)
-        accs = [bank("acc1%d" % jb, acc_tags[1][jb], [P, N]) for jb in range(blocks)]
-        gated = [tile("pt1%d" % jb, [P, PACK, P], F32) for jb in range(blocks)]
-        products(1, range(blocks))
-        gate(1, range(blocks), 0, PACK)
-        for s in range(PACK):
-            turn(1, s, range(blocks), acc_tags[0][s])
+        every_block = range(BLOCKS)
+        halves = (every_block[: BLOCKS // 2], every_block[BLOCKS // 2 :])
+        accs_a = [bank("acc_a%d" % b, 4 + b, [P, N]) for b in every_block]
+        by_token_a = [tile("by_token_a%d" % b, [P, SLOTS, P], F32) for b in every_block]
+        for h, half in enumerate(halves):
+            expert_products(A, half, accs_a)
+            gate(A, half, accs_a, by_token_a, 0, 1)
+            turn(A, 0, half, by_token_a, h)
+        gate(A, every_block, accs_a, by_token_a, 1, SLOTS)
+        for s in range(1, SLOTS):
+            turn(A, s, every_block, by_token_a, s - 1)
+        accs_b = []
+        by_token_b = [tile("by_token_b%d" % b, [P, SLOTS, P], F32) for b in every_block]
+        for b in every_block:
+            accs_b.append(bank("acc_b%d" % b, b % (SLOTS - 1), [P, N]))
+            expert_products(B, (b,), accs_b)
+            gate(B, (b,), accs_b, by_token_b, 0, SLOTS)
+        for s in range(SLOTS):
+            turn(B, s, every_block, by_token_b, 4 + s)
 
-        def scatter(e, s):
-            nc.vector.tensor_copy(windows[e][s % 2][:].indirect(lists[e][:]), srcs[e][s][:])
+        def scatter(e, s, first=0, count=J):
+            nc.vector.tensor_copy(
+                windows[e][s % 2][:].indirect(lists[e][:, first // PER_COLUMN : (first + count) // PER_COLUMN]),
+                gated_slots[e][s][:, first : first + count],
+            )
 
-        def onto_res(e, s, cols):
+        def first_sum(e, s, cols):
             nc.gpsimd.tensor_tensor(out=sums[s][:, cols], in0=windows[e][s % 2][:, cols], in1=sums[s][:, cols], op=ADD)
 
-        def finish(e, s, cols):
-            nc.gpsimd.tensor_tensor(
-                out=pairs[s // 2][:, s % 2, cols], in0=windows[e][s % 2][:, cols], in1=sums[s][:, cols], op=ADD
+        def second_sum(engine, e, s, cols):
+            engine.tensor_tensor(
+                out=h_pairs[s // 2][:, s % 2, cols], in0=windows[e][s % 2][:, cols], in1=sums[s][:, cols], op=ADD
             )
 
-        every, early, late = slice(0, T), slice(0, EARLY), slice(EARLY, T)
-        for h in range(2):
-            nc.vector.tensor_copy(
-                windows[0][0][:].indirect(lists[0][:, 16 * h : 16 * h + 16]), srcs[0][0][:, 256 * h : 256 * h + 256]
-            )
-        onto_res(0, 0, every)
-        scatter(0, 1)
-        onto_res(0, 1, early)
-        scatter(0, 2)
-        onto_res(0, 2, every)
-        scatter(1, 0)
-        finish(1, 0, every)
-        scatter(1, 1)
-        finish(1, 1, early)
-        onto_res(1, 1, late)
-        finish(0, 1, late)
-        for c in range(CHUNKS):
-            cols = slice(STARTS[c], STARTS[c] + WIDTHS[c])
+        def relu_pair_on_scalar(pair, c):
             nc.scalar.activation(
-                out=grouped[c][:, :, 0:2], in_=pairs[0][:, :, cols].rearrange("p e c -> p c e"), func=RELU
+                out=h_grouped[c][:, :, 2 * pair : 2 * pair + 2],
+                in_=h_pairs[pair][:, :, chunk(c)].rearrange("p s t -> p t s"),
+                func=RELU,
             )
-        scatter(1, 2)
-        finish(1, 2, every)
-        scatter(1, 3)
-        warm = bank("warm", "m3", [P, N])
-        for lo, hi, count in ((0, 0, 1), (0, 512, 2), (512, T, 2)):
-            if hi > lo:
-                onto_res(1, 3, slice(lo, hi))
-            nc.tensor.transpose(warm[:, 0:P], sums[3][:, hi - P : hi] if hi > lo else windows[1][1][:, 0:P], ident[:])
-            for i in range(count):
-                nc.tensor.matmul_mx(
-                    out=warm[:],
-                    lhsT=g_words[0][0][:, 0:P].bitcast(FP4X4),
-                    lhsT_scale=g_scales[0][0][:, 0:P],
-                    rhs=w_ops[0][0],
-                    rhs_scale=w_scales[0][:, 0, :],
-                    start=True,
-                    stop=True,
-                )
-        scatter(0, 3)
 
-        last = windows[0][(PACK - 1) % 2]
-        y_tags = ["t0", "t1", "t2", "t3", "m0", "m1", "m2", "m3"]
-        used = []
-        out_rows = out_0.rearrange("(p s) t -> p s t", s=PACK)
-        out_words = out_1.rearrange("z p c r -> p (z c r)").bitcast(I32)
-        y_scales = tile("y_scales", [P, T], U8)
+        all_tokens, a_first, b_first = slice(0, T), slice(0, A_FIRST), slice(A_FIRST, T)
+        scatter(A, 0, 0, J // 2)
+        scatter(A, 0, J // 2, J // 2)
+        first_sum(A, 0, all_tokens)
+        scatter(A, 1)
+        first_sum(A, 1, a_first)
+        scatter(A, 2)
+        first_sum(A, 2, all_tokens)
+        scatter(B, 0)
+        second_sum(nc.gpsimd, B, 0, all_tokens)
+        scatter(B, 1)
+        second_sum(nc.gpsimd, B, 1, a_first)
+        first_sum(B, 1, b_first)
+        second_sum(nc.gpsimd, A, 1, b_first)
+        for c in range(LAST + 1):
+            relu_pair_on_scalar(0, c)
+        scatter(B, 2)
+        second_sum(nc.gpsimd, B, 2, all_tokens)
+        scatter(B, 3)
+        first_sum(B, 3, all_tokens)
+        scatter(A, 3)
+
+        out_slots = out_0.rearrange("(p s) t -> p s t", s=SLOTS)
+        out_words = out_1.rearrange("z p t r -> p (z t r)").bitcast(I32)
+        y_plane = tile("y_plane", [P, T], U8)
         y_words = tile("y_words", [P, T], I32)
-        hq = []
+        h_quantised, y_chunks, y_grouped, banks_taken = {}, {}, {}, []
 
-        def front(c):
-            cols = slice(STARTS[c], STARTS[c] + WIDTHS[c])
-            src = pairs[1][:, :, cols].rearrange("p e c -> p c e")
-            if c in SCALAR_FRONT:
-                nc.scalar.activation(out=grouped[c][:, :, 2:4], in_=src, func=RELU)
-            elif c == 3:
-                src = pairs[1][:, :, STARTS[3] : T].rearrange("p e c -> p c e")
-                nc.vector.tensor_scalar(out=tail_group[:, :, 2:4], in0=src, scalar1=0.0, scalar2=None, op0=MAX)
-            else:
-                nc.vector.tensor_scalar(out=grouped[c][:, :, 2:4], in0=src, scalar1=0.0, scalar2=None, op0=MAX)
+        def last_sum(first, end):
+            second_sum(nc.vector, A, SLOTS - 1, slice(first, end))
 
-        def quant(c):
-            words = tile("hq%d" % c, [P, WIDTHS[c]], I32)
-            scales = tile("hs%d" % c, [P, WIDTHS[c]], U8)
-            nc.vector.quantize_mx(
-                out=words[:].bitcast(FP8X4), scales=scales[:], in_=grouped[c].rearrange("p c s -> p (c s)")
+        def relu_pair_on_vector(grouped, cols):
+            nc.vector.tensor_scalar(
+                out=grouped[:, :, 2:4], in0=h_pairs[1][:, :, cols].rearrange("p s t -> p t s"),
+                scalar1=0.0, scalar2=None, op0=MAX,
             )
-            hq.append((words, scales))
 
-        def add(lo, hi):
-            cols = slice(lo, hi)
-            nc.vector.tensor_tensor(out=pairs[1][:, 1, cols], in0=last[:, cols], in1=sums[PACK - 1][:, cols], op=ADD)
+        def quantise_h(c):
+            words = tile("h_words%d" % c, [P, WIDTHS[c]], I32)
+            plane = tile("h_plane%d" % c, [P, WIDTHS[c]], U8)
+            nc.vector.quantize_mx(
+                out=words[:].bitcast(FP8X4), scales=plane[:], in_=h_grouped[c].rearrange("p t s -> p (t s)")
+            )
+            h_quantised[c] = (words, plane)
 
-        ys = []
-        ybs = {}
-
-        def product(c):
-            cols = slice(STARTS[c], STARTS[c] + WIDTHS[c])
-            words, scales = hq[c]
-            y = tile("y%d" % c, [P, PACK, WIDTHS[c]], F32)
-            per_bank = 512 // WIDTHS[c]
-            for s0 in range(0, PACK, per_bank):
-                acc = bank("yacc%d%d" % (c, s0), y_tags[len(used)], [P, per_bank, WIDTHS[c]])
-                used.append(c)
+        def shared_product(c):
+            words, plane = h_quantised[c]
+            y = tile("y%d" % c, [P, SLOTS, WIDTHS[c]], F32)
+            per_bank = BANK // WIDTHS[c]
+            for s0 in range(0, SLOTS, per_bank):
+                acc = bank("y_acc%d%d" % (c, s0), len(banks_taken), [P, per_bank, WIDTHS[c]])
+                banks_taken.append(c)
                 for i in range(per_bank):
-                    s = s0 + i
+                    rows = slice((s0 + i) * P, (s0 + i + 1) * P)
                     nc.tensor.matmul_mx(
                         out=acc[:, i, :],
-                        lhsT=wmp[:, s * P : (s + 1) * P].bitcast(FP8X4),
-                        lhsT_scale=wmsp[:, s * P : (s + 1) * P],
+                        lhsT=wm_sorted[:, rows].bitcast(FP8X4),
+                        lhsT_scale=wm_plane_sorted[:, rows],
                         rhs=words[:].bitcast(FP8X4),
-                        rhs_scale=scales[:],
+                        rhs_scale=plane[:],
                         start=True,
                         stop=True,
                     )
-                if c in PSUM_ROUND:
-                    yb = tile("yb%d" % c, [P, WIDTHS[c], PACK], BF16)
-                    nc.scalar.copy(out=yb[:], in_=acc[:].rearrange("p s c -> p c s"))
-                    ybs[c] = yb
+                if c == LAST:
+                    y_grouped[c] = tile("y_grouped%d" % c, [P, WIDTHS[c], SLOTS], BF16)
+                    nc.scalar.copy(out=y_grouped[c][:], in_=acc[:].rearrange("p s t -> p t s"))
                 nc.scalar.copy(out=y[:, s0 : s0 + per_bank, :], in_=acc[:])
-                if c != 3:
-                    nc.sync.dma_start(out=out_rows[:, s0 : s0 + per_bank, cols], in_=y[:, s0 : s0 + per_bank, :])
-            if c == 3:
-                nc.sync.dma_start(out=out_rows[:, :, cols], in_=y[:])
-            ys.append(y)
-
+                if c != LAST - 1:
+                    nc.sync.dma_start(out=out_slots[:, s0 : s0 + per_bank, chunk(c)], in_=y[:, s0 : s0 + per_bank, :])
+            if c == LAST - 1:
+                nc.sync.dma_start(out=out_slots[:, :, chunk(c)], in_=y[:])
+            y_chunks[c] = y
 
         def round_y(c):
-            yb = tile("yb%d" % c, [P, WIDTHS[c], PACK], BF16)
+            y_grouped[c] = tile("y_grouped%d" % c, [P, WIDTHS[c], SLOTS], BF16)
             nc.vector.tensor_copy(
-                out=yb[:].rearrange("p (c i) s -> p c s i", i=4), in_=ys[c][:].rearrange("p s (c i) -> p c s i", i=4)
+                out=y_grouped[c][:].rearrange("p (t i) s -> p t s i", i=LINE),
+                in_=y_chunks[c][:].rearrange("p s (t i) -> p t s i", i=LINE),
             )
-            ybs[c] = yb
 
-        def planes(c):
-            cols = slice(STARTS[c], STARTS[c] + WIDTHS[c])
+        def quantise_y(c):
             nc.vector.quantize_mx(
-                out=y_words[:, cols].bitcast(FP8X4), scales=y_scales[:, cols], in_=ybs[c][:].rearrange("p c s -> p (c s)")
+                out=y_words[:, chunk(c)].bitcast(FP8X4),
+                scales=y_plane[:, chunk(c)],
+                in_=y_grouped[c][:].rearrange("p t s -> p (t s)"),
             )
 
         def store_words(c0, c1):
             cols = slice(STARTS[c0], STARTS[c1] + WIDTHS[c1])
             nc.sync.dma_start(out=out_words[:, cols], in_=y_words[:, cols])
 
-        add(0, 128)
-        add(128, 256)
-        front(0)
-        add(256, 384)
-        front(1)
-        quant(0)
-        product(0)
-        add(384, 640)
-        front(2)
-        add(640, 1024)
-        quant(1)
-        product(1)
-        front(3)
-        quant(2)
-        product(2)
-        quant(3)
-        product(3)
-        quant(4)
-        product(4)
+        middle = STARTS[1] + WIDTHS[1] // 2
+        last_sum(0, STARTS[1])
+        last_sum(STARTS[1], middle)
+        relu_pair_on_vector(h_grouped[0], chunk(0))
+        last_sum(middle, STARTS[2])
+        relu_pair_on_scalar(1, 1)
+        quantise_h(0)
+        shared_product(0)
+        last_sum(STARTS[2], STARTS[3])
+        relu_pair_on_scalar(1, 2)
+        last_sum(STARTS[3], T)
+        quantise_h(1)
+        shared_product(1)
+        relu_pair_on_vector(h_grouped_end[:], slice(STARTS[LAST - 1], T))
+        for c in range(2, LAST + 1):
+            quantise_h(c)
+            shared_product(c)
         round_y(0)
         round_y(1)
-        planes(0)
+        quantise_y(0)
         round_y(2)
-        planes(1)
+        quantise_y(1)
         store_words(0, 1)
         round_y(3)
-        planes(2)
+        quantise_y(2)
         store_words(2, 2)
-        planes(4)
-        planes(3)
-        store_words(3, 4)
+        quantise_y(LAST)
+        quantise_y(3)
+        store_words(3, LAST)
         for q in range(QUADS):
-            (nc.scalar if q % 2 else nc.sync).dma_start(
-                out=out_2[0, 4 * q : 4 * q + 4, :].bitcast(I32), in_=y_scales[32 * q : 32 * q + 4, :].bitcast(I32)
+            queue = nc.scalar if q % 2 else nc.sync
+            queue.dma_start(
+                out=out_2[0, 4 * q : 4 * q + 4, :].bitcast(I32), in_=y_plane[32 * q : 32 * q + 4, :].bitcast(I32)
             )

from contextlib import ExitStack

import concourse.mybir as mybir
from concourse.masks import make_identity

K, T, J, N, M = 1024, 1024, 512, 512, 512
FLOPS = 2 * (2 * K * N * J + N * M * T)

F32 = mybir.dt.float32
BF16 = mybir.dt.bfloat16
I32 = mybir.dt.int32
U16 = mybir.dt.uint16
U8 = mybir.dt.uint8
FP8X4 = mybir.dt.float8_e4m3fn_x4
FP4X4 = mybir.dt.float4_e2m1fn_x4
ADD = mybir.AluOpType.add
MAX = mybir.AluOpType.max
COPY = mybir.ActivationFunctionType.Copy
RELU = mybir.ActivationFunctionType.Relu

P = 128
SLOTS = 4
PASSES = K // (P * SLOTS)
QUADS = 4
BLOCKS = J // P
PER_COLUMN = 16
BANK = 512
LINE = 4
A, B = 0, 1

WIDTHS = (128, 256, 256, 256, 128)
STARTS = tuple(sum(WIDTHS[:c]) for c in range(len(WIDTHS)))
LAST = len(WIDTHS) - 1
A_FIRST = 768


def tile_moe_experts_then_shared_layer_pl_kernel(
    tc, xt_words, xt_scales, wa_words, wa_scales, wb_words, wb_scales, res, wm_words, wm_scales, ga, gb, offs, offs2,
    out_0, out_1, out_2,
):
    nc = tc.nc
    with ExitStack() as ctx:
        sb = ctx.enter_context(tc.tile_pool(name="sb", bufs=1))
        ps = ctx.enter_context(tc.psum_pool(name="ps", bufs=1))

        def tile(name, shape, dtype):
            return sb.tile(shape, dtype, name=name, align_bytes=64)

        def bank(name, number, shape):
            return ps.tile(shape, F32, name=name, tag="bank%d" % number)

        def chunk(c):
            return slice(STARTS[c], STARTS[c] + WIDTHS[c])

        def zeroed_plane(name, shape, engine):
            plane = tile(name, shape, U8)
            engine.memset(plane[:].bitcast(I32), 0)
            return plane

        def load_weight_scales(plane, scales):
            for q in range(QUADS):
                nc.sync.dma_start(
                    out=plane[32 * q : 32 * q + 4, :, :].bitcast(I32),
                    in_=scales[:, 4 * q : 4 * q + 4, :].rearrange("a r n -> r a n").bitcast(I32),
                )

        def load_gate(name, gate_row):
            gate_tile = tile(name, [P, BLOCKS], F32)
            with nc.allow_non_contiguous_dma(reason="one gate to a partition"):
                nc.sync.dma_start(out=gate_tile[:], in_=gate_row.rearrange("o (b p) -> p (o b)", p=P))
            return gate_tile

        lists = [tile("list_a", [P, J // PER_COLUMN], U16), tile("list_b", [P, J // PER_COLUMN], U16)]
        x_scales = zeroed_plane("x_scales", [P, T], nc.gpsimd)
        wa_plane = zeroed_plane("wa_plane", [P, PASSES, N], nc.gpsimd)
        moved = [zeroed_plane("moved_a", [P, J], nc.vector), zeroed_plane("moved_b", [P, J], nc.vector)]
        wm_plane = zeroed_plane("wm_plane", [P, 1, M], nc.vector)
        wb_plane = zeroed_plane("wb_plane", [P, PASSES, N], nc.vector)

        ident = tile("ident", [P, P], F32)
        make_identity(nc, ident[:])
        windows = [[tile("window%d%d" % (e, i), [P, T], F32) for i in range(2)] for e in (A, B)]
        for e in (A, B):
            for window in windows[e]:
                nc.gpsimd.memset(window[:], 0.0)

        x_words = [tile("x_words%d" % a, [P, T], U16) for a in range(PASSES)]
        wa = tile("wa", [P, PASSES, N], I32)
        nc.sync.dma_start(lists[A][:], offs)
        nc.sync.dma_start(out=x_words[0][:].bitcast(I32), in_=xt_words[0].bitcast(I32))
        for q in range(QUADS):
            nc.sync.dma_start(
                out=x_scales[32 * q : 32 * q + 4 * PASSES, :].bitcast(I32),
                in_=xt_scales[:, 4 * q : 4 * q + 4, :].bitcast(I32),
            )
        nc.sync.dma_start(out=x_words[1][:].bitcast(I32), in_=xt_words[1].bitcast(I32))
        nc.sync.dma_start(out=wa[:], in_=wa_words.rearrange("a p n r -> p a (n r)").bitcast(I32))
        load_weight_scales(wa_plane, wa_scales)
        nc.sync.dma_start(lists[B][:], offs2)
        gates = [load_gate("gate_a", ga)]

        picked_words = [[tile("picked%d%d" % (e, a), [P, J], U16) for a in range(PASSES)] for e in (A, B)]
        picked_planes = [[tile("picked_scales%d" % e, [P, J], U8), moved[e]] for e in (A, B)]

        def gather_words(e, a):
            nc.vector.tensor_copy(picked_words[e][a][:], x_words[a][:].indirect(lists[e][:]))

        def gather_scales(e):
            both = picked_planes[e][0]
            nc.vector.tensor_copy(both[:], x_scales[:].indirect(lists[e][:]))
            for first, rows in ((0, 64), (64, 4), (96, 4)):
                nc.sync.dma_start(
                    out=moved[e][first : first + rows, :].bitcast(I32),
                    in_=both[first + 4 : first + 4 + rows, :].bitcast(I32),
                )

        gather_words(A, 0)
        gather_scales(A)
        gather_words(A, 1)
        wm = tile("wm", [P, M], I32)
        nc.sync.dma_start(out=wm[:], in_=wm_words[0].rearrange("p m r -> p (m r)").bitcast(I32))
        load_weight_scales(wm_plane, wm_scales)
        gather_scales(B)
        gather_words(B, 0)
        gather_words(B, 1)
        load_weight_scales(wb_plane, wb_scales)
        wb = tile("wb", [P, PASSES, N // 2], I32)
        nc.sync.dma_start(out=wb[:], in_=wb_words.rearrange("a p n -> p a n").bitcast(I32))
        res_slots = res.rearrange("(p s) t -> p s t", s=SLOTS)
        sums = [tile("sum%d" % s, [P, T], F32) for s in range(SLOTS)]
        nc.sync.dma_start(out=sums[0][:], in_=res_slots[:, 0, :])
        gates.append(load_gate("gate_b", gb))
        for s in range(1, SLOTS):
            nc.sync.dma_start(out=sums[s][:], in_=res_slots[:, s, :])

        wm_sorted = tile("wm_sorted", [P, M], I32)
        nc.vector.tensor_copy(
            out=wm_sorted[:].rearrange("p (s i) -> p i s", s=SLOTS), in_=wm[:].rearrange("p (i s) -> p i s", s=SLOTS)
        )
        wm_plane_sorted = tile("wm_plane_sorted", [P, M], U8)
        nc.vector.tensor_copy(
            out=wm_plane_sorted[:].rearrange("p (s i) -> p s i", s=SLOTS),
            in_=wm_plane[:, 0, :].rearrange("p (i s) -> p s i", s=SLOTS),
        )

        w_words = [
            [wa[:, a, :].bitcast(FP8X4) for a in range(PASSES)],
            [wb[:, a, :].bitcast(FP4X4) for a in range(PASSES)],
        ]
        w_planes = [wa_plane, wb_plane]
        h_pairs = [tile("h_slots01", [P, 2, T], BF16), tile("h_slots23", [P, 2, T], BF16)]
        h_grouped = [tile("h_grouped%d" % c, [P, WIDTHS[c], SLOTS], BF16)[:] for c in range(LAST - 1)]
        h_grouped_end = tile("h_grouped_end", [P, WIDTHS[LAST - 1] + WIDTHS[LAST], SLOTS], BF16)
        h_grouped.append(h_grouped_end[:, 0 : WIDTHS[LAST - 1], :])
        h_grouped.append(h_grouped_end[:, WIDTHS[LAST - 1] :, :])
        gated_slots = [[tile("gated%d%d" % (e, s), [P, J], F32) for s in range(SLOTS)] for e in (A, B)]

        def expert_products(e, blocks, accs):
            for a in range(PASSES):
                for b in blocks:
                    tokens = slice(b * P, (b + 1) * P)
                    nc.tensor.matmul_mx(
                        out=accs[b][:],
                        lhsT=picked_words[e][a][:, tokens].bitcast(FP4X4),
                        lhsT_scale=picked_planes[e][a][:, tokens],
                        rhs=w_words[e][a],
                        rhs_scale=w_planes[e][:, a, :],
                        start=(a == 0),
                        stop=(a == PASSES - 1),
                    )

        def gate(e, blocks, accs, by_token, s0, s1):
            for b in blocks:
                nc.scalar.activation(
                    out=by_token[b][:, s0:s1, :],
                    in_=accs[b][:].rearrange("j (i s) -> j s i", s=SLOTS)[:, s0:s1, :],
                    func=COPY,
                    scale=gates[e][:, b : b + 1],
                )

        def turn(e, s, blocks, by_token, number):
            turned = bank("turned%d%d%d" % (e, s, blocks[0]), number, [P, len(blocks) * P])
            for i, b in enumerate(blocks):
                nc.tensor.transpose(turned[:, i * P : (i + 1) * P], by_token[b][:, s, :], ident[:])
            nc.scalar.copy(out=gated_slots[e][s][:, blocks[0] * P : (blocks[-1] + 1) * P], in_=turned[:])

        every_block = range(BLOCKS)
        halves = (every_block[: BLOCKS // 2], every_block[BLOCKS // 2 :])
        accs_a = [bank("acc_a%d" % b, 4 + b, [P, N]) for b in every_block]
        by_token_a = [tile("by_token_a%d" % b, [P, SLOTS, P], F32) for b in every_block]
        for h, half in enumerate(halves):
            expert_products(A, half, accs_a)
            gate(A, half, accs_a, by_token_a, 0, 1)
            turn(A, 0, half, by_token_a, h)
        gate(A, every_block, accs_a, by_token_a, 1, SLOTS)
        for s in range(1, SLOTS):
            turn(A, s, every_block, by_token_a, s - 1)
        accs_b = []
        by_token_b = [tile("by_token_b%d" % b, [P, SLOTS, P], F32) for b in every_block]
        for b in every_block:
            accs_b.append(bank("acc_b%d" % b, b % (SLOTS - 1), [P, N]))
            expert_products(B, (b,), accs_b)
            gate(B, (b,), accs_b, by_token_b, 0, SLOTS)
        for s in range(SLOTS):
            turn(B, s, every_block, by_token_b, 4 + s)

        def scatter(e, s, first=0, count=J):
            nc.vector.tensor_copy(
                windows[e][s % 2][:].indirect(lists[e][:, first // PER_COLUMN : (first + count) // PER_COLUMN]),
                gated_slots[e][s][:, first : first + count],
            )

        def first_sum(e, s, cols):
            nc.gpsimd.tensor_tensor(out=sums[s][:, cols], in0=windows[e][s % 2][:, cols], in1=sums[s][:, cols], op=ADD)

        def second_sum(engine, e, s, cols):
            engine.tensor_tensor(
                out=h_pairs[s // 2][:, s % 2, cols], in0=windows[e][s % 2][:, cols], in1=sums[s][:, cols], op=ADD
            )

        def relu_pair_on_scalar(pair, c):
            nc.scalar.activation(
                out=h_grouped[c][:, :, 2 * pair : 2 * pair + 2],
                in_=h_pairs[pair][:, :, chunk(c)].rearrange("p s t -> p t s"),
                func=RELU,
            )

        all_tokens, a_first, b_first = slice(0, T), slice(0, A_FIRST), slice(A_FIRST, T)
        scatter(A, 0, 0, J // 2)
        scatter(A, 0, J // 2, J // 2)
        first_sum(A, 0, all_tokens)
        scatter(A, 1)
        first_sum(A, 1, a_first)
        scatter(A, 2)
        first_sum(A, 2, all_tokens)
        scatter(B, 0)
        second_sum(nc.gpsimd, B, 0, all_tokens)
        scatter(B, 1)
        second_sum(nc.gpsimd, B, 1, a_first)
        first_sum(B, 1, b_first)
        second_sum(nc.gpsimd, A, 1, b_first)
        for c in range(LAST + 1):
            relu_pair_on_scalar(0, c)
        scatter(B, 2)
        second_sum(nc.gpsimd, B, 2, all_tokens)
        scatter(B, 3)
        first_sum(B, 3, all_tokens)
        scatter(A, 3)

        out_slots = out_0.rearrange("(p s) t -> p s t", s=SLOTS)
        out_words = out_1.rearrange("z p t r -> p (z t r)").bitcast(I32)
        y_plane = tile("y_plane", [P, T], U8)
        y_words = tile("y_words", [P, T], I32)
        h_quantised, y_chunks, y_grouped, banks_taken = {}, {}, {}, []

        def last_sum(first, end):
            second_sum(nc.vector, A, SLOTS - 1, slice(first, end))

        def relu_pair_on_vector(grouped, cols):
            nc.vector.tensor_scalar(
                out=grouped[:, :, 2:4], in0=h_pairs[1][:, :, cols].rearrange("p s t -> p t s"),
                scalar1=0.0, scalar2=None, op0=MAX,
            )

        def quantise_h(c):
            words = tile("h_words%d" % c, [P, WIDTHS[c]], I32)
            plane = tile("h_plane%d" % c, [P, WIDTHS[c]], U8)
            nc.vector.quantize_mx(
                out=words[:].bitcast(FP8X4), scales=plane[:], in_=h_grouped[c].rearrange("p t s -> p (t s)")
            )
            h_quantised[c] = (words, plane)

        def shared_product(c):
            words, plane = h_quantised[c]
            y = tile("y%d" % c, [P, SLOTS, WIDTHS[c]], F32)
            per_bank = BANK // WIDTHS[c]
            for s0 in range(0, SLOTS, per_bank):
                acc = bank("y_acc%d%d" % (c, s0), len(banks_taken), [P, per_bank, WIDTHS[c]])
                banks_taken.append(c)
                for i in range(per_bank):
                    rows = slice((s0 + i) * P, (s0 + i + 1) * P)
                    nc.tensor.matmul_mx(
                        out=acc[:, i, :],
                        lhsT=wm_sorted[:, rows].bitcast(FP8X4),
                        lhsT_scale=wm_plane_sorted[:, rows],
                        rhs=words[:].bitcast(FP8X4),
                        rhs_scale=plane[:],
                        start=True,
                        stop=True,
                    )
                if c == LAST:
                    y_grouped[c] = tile("y_grouped%d" % c, [P, WIDTHS[c], SLOTS], BF16)
                    nc.scalar.copy(out=y_grouped[c][:], in_=acc[:].rearrange("p s t -> p t s"))
                nc.scalar.copy(out=y[:, s0 : s0 + per_bank, :], in_=acc[:])
                if c != LAST - 1:
                    nc.sync.dma_start(out=out_slots[:, s0 : s0 + per_bank, chunk(c)], in_=y[:, s0 : s0 + per_bank, :])
            if c == LAST - 1:
                nc.sync.dma_start(out=out_slots[:, :, chunk(c)], in_=y[:])
            y_chunks[c] = y

        def round_y(c):
            y_grouped[c] = tile("y_grouped%d" % c, [P, WIDTHS[c], SLOTS], BF16)
            nc.vector.tensor_copy(
                out=y_grouped[c][:].rearrange("p (t i) s -> p t s i", i=LINE),
                in_=y_chunks[c][:].rearrange("p s (t i) -> p t s i", i=LINE),
            )

        def quantise_y(c):
            nc.vector.quantize_mx(
                out=y_words[:, chunk(c)].bitcast(FP8X4),
                scales=y_plane[:, chunk(c)],
                in_=y_grouped[c][:].rearrange("p t s -> p (t s)"),
            )

        def store_words(c0, c1):
            cols = slice(STARTS[c0], STARTS[c1] + WIDTHS[c1])
            nc.sync.dma_start(out=out_words[:, cols], in_=y_words[:, cols])

        middle = STARTS[1] + WIDTHS[1] // 2
        last_sum(0, STARTS[1])
        last_sum(STARTS[1], middle)
        relu_pair_on_vector(h_grouped[0], chunk(0))
        last_sum(middle, STARTS[2])
        relu_pair_on_scalar(1, 1)
        quantise_h(0)
        shared_product(0)
        last_sum(STARTS[2], STARTS[3])
        relu_pair_on_scalar(1, 2)
        last_sum(STARTS[3], T)
        quantise_h(1)
        shared_product(1)
        relu_pair_on_vector(h_grouped_end[:], slice(STARTS[LAST - 1], T))
        for c in range(2, LAST + 1):
            quantise_h(c)
            shared_product(c)
        round_y(0)
        round_y(1)
        quantise_y(0)
        round_y(2)
        quantise_y(1)
        store_words(0, 1)
        round_y(3)
        quantise_y(2)
        store_words(2, 2)
        quantise_y(LAST)
        quantise_y(3)
        store_words(3, LAST)
        for q in range(QUADS):
            queue = nc.scalar if q % 2 else nc.sync
            queue.dma_start(
                out=out_2[0, 4 * q : 4 * q + 4, :].bitcast(I32), in_=y_plane[32 * q : 32 * q + 4, :].bitcast(I32)
            )
